import numpy as np
import ml_dtypes


def mxq(x, axis, fmt="e4m3"):
    dtype, down = {"e4m3": (ml_dtypes.float8_e4m3fn, 7), "e5m2": (ml_dtypes.float8_e5m2, 14)}[fmt]
    v = np.moveaxis(np.asarray(x, np.float32).astype(ml_dtypes.bfloat16).astype(np.float64), axis, -1)
    blocks = v.reshape(v.shape[:-1] + (-1, 32))
    amax = np.abs(blocks).max(-1, keepdims=True)
    byte = np.maximum(np.where(amax > 0, np.frexp(amax)[1] - 1 + 127, 0) - down, 1)
    scale = np.exp2(byte - 127.0)
    codes = (blocks / scale).astype(np.float32).astype(dtype).astype(np.float64)
    return np.moveaxis((codes * scale).reshape(v.shape), -1, axis)


WIDE = False


def mx_kscale(k):
    if not WIDE:
        return np.ones(k)
    levels = np.array([10, -10, 5, -5, 0])
    if k % 512:
        return np.exp2(np.random.permutation(np.resize(levels, k // 32))).repeat(32)
    a = np.empty((k // 512, 16))
    for p in range(k // 512):
        a[p, :8] = np.random.permutation(np.resize(levels, 8))
        for g in range(8):
            far = levels[np.abs(levels - a[p, g]) >= 10]
            a[p, g + 8] = far[np.random.randint(len(far))]
    return np.exp2(a.ravel()).repeat(32)


def f64(x):
    return np.asarray(x).astype(np.float64)


def striped(idx):
    return np.tile(idx.reshape(-1, 16).T, (8, 1)).astype(np.uint16)


def unstriped(offs):
    return offs[:16].T.reshape(-1).astype(np.int64)


def pack_weight(w):
    k, n = w.shape
    w = f64(np.asarray(w, np.float32).astype(ml_dtypes.bfloat16)).reshape(k // 32, 32, n)
    amax = np.abs(w).max(1)
    byte = np.clip(np.where(amax > 0, np.frexp(amax)[1] - 1 + 127 - 7, 1), 1, 254)
    scaled = (w * np.exp2(127.0 - byte)[:, None, :]).reshape(k, n).astype(np.float32)
    words = np.ascontiguousarray(scaled.reshape(k // 512, 128, 4, n).transpose(0, 1, 3, 2)).astype(ml_dtypes.float8_e4m3fn).view(np.uint8)
    return words, np.ascontiguousarray(byte.astype(np.uint8).reshape(k // 512, 16, n))


def unpack_weight(words, scales):
    g, p, n, _ = words.shape
    vals = np.ascontiguousarray(words).view(ml_dtypes.float8_e4m3fn).astype(np.float64) * np.repeat(np.exp2(scales.astype(np.float64) - 127.0), 8, axis=1)[..., None]
    return vals.transpose(0, 1, 3, 2).reshape(g * 512, n)

def planes(y):
    n, m = y.shape
    v = y.astype(np.float32).astype(ml_dtypes.bfloat16).astype(np.float64).reshape(n // 32, 32, m)
    top = np.abs(v).max(1)
    byte = np.clip(np.where(top > 0, np.frexp(top)[1] - 1 + 127 - 7, 1), 1, 254)
    codes = (v * np.exp2(127.0 - byte)[:, None, :]).reshape(n, m).astype(np.float32).astype(ml_dtypes.float8_e4m3fn).view(np.uint8)
    words = codes.reshape(n // 512, 128, 4, m).transpose(0, 1, 3, 2)
    return np.ascontiguousarray(words), np.ascontiguousarray(byte.astype(np.uint8).reshape(n // 512, 16, m))


K, T, S, V, N = 512, 1024, 512, 256, 512


def setup_inputs():
    n = np.random.standard_normal
    s = mx_kscale(K)[:, None]
    packed_xT = pack_weight(n((K, T)) * s)
    return {
        "x_words": packed_xT[0],
        "x_scales": packed_xT[1],
        "w1": (n((K, N)) / np.sqrt(K) / s).astype(np.float32),
        "offs": striped(np.random.permutation(T)[:S]),
        "pos1": striped(np.random.permutation(S)[:V]),
        "pos2": striped(np.random.permutation(S)[:V]),
        "pos3": striped(np.random.permutation(S)[:V]),
    }


def reference(x_words, x_scales, w1, offs, pos1, pos2, pos3):
    xq = unpack_weight(x_words, x_scales)[:, unstriped(offs)]
    y = mxq(f64(w1), 0, "e4m3").T @ xq
    n0 = y[:, unstriped(pos1)]
    n1 = y[:, unstriped(pos2)]
    n2 = y[:, unstriped(pos3)]
    out_0 = np.maximum(np.minimum(n0, n1), np.minimum(np.maximum(n0, n1), n2))
    return (out_0,) + planes(out_0)

@@ -1,0 +1,213 @@
+from contextlib import ExitStack
+
+import concourse.mybir as mybir
+
+K, T, S, V, N = 512, 1024, 512, 256, 512
+FLOPS = 2 * K * N * S
+
+F32 = mybir.dt.float32
+BF16 = mybir.dt.bfloat16
+I32 = mybir.dt.int32
+U32 = mybir.dt.uint32
+U16 = mybir.dt.uint16
+U8 = mybir.dt.uint8
+FP8X4 = mybir.dt.float8_e4m3fn_x4
+COPY = mybir.ActivationFunctionType.Copy
+MAX = mybir.AluOpType.max
+MIN = mybir.AluOpType.min
+
+P = 128
+PACK = 4
+LANES = 16
+HALF_S = S // 2
+HALF_N = N // 2
+HALF_P = P // 2
+HALF_V = V // 2
+VECTOR_SHARE = 40
+
+
+def tile_picked_median_none_po_kernel(
+    tc, x_words, x_scales, w1, offs, pos1, pos2, pos3, out_0, out_1, out_2
+):
+    nc = tc.nc
+    with ExitStack() as ctx:
+        keep = ctx.enter_context(tc.tile_pool(name="keep", bufs=1))
+        psum = ctx.enter_context(tc.psum_pool(name="psum", bufs=1))
+
+        def sbuf(shape, dtype, name):
+            return keep.tile(shape, dtype, name=name, align_bytes=64)
+
+        picked = keep.tile([P, S // LANES], U16, name="picked")
+        places = [keep.tile([P, V // LANES], U16, name="places%d" % i) for i in range(3)]
+        table_words = sbuf([P, T], U32, "table_words")
+        table_scales = sbuf([P, T], U8, "table_scales")
+        w_raw = [sbuf([P, PACK, HALF_N], F32, "w_raw%d" % h) for h in range(2)]
+
+        nc.vector.memset(table_scales[:].bitcast(I32), 0)
+        nc.sync.dma_start(picked[:], offs)
+        w_rows = w1.rearrange("(p j) c -> p j c", j=PACK)
+        nc.sync.dma_start(w_raw[0][:], w_rows[:, :, :HALF_N])
+        for q in range(4):
+            nc.sync.dma_start(
+                table_scales[32 * q : 32 * q + 4, :].bitcast(I32),
+                x_scales[0, 4 * q : 4 * q + 4, :].bitcast(I32),
+            )
+        nc.sync.dma_start(w_raw[1][:], w_rows[:, :, HALF_N:])
+        nc.sync.dma_start(
+            table_words[:].bitcast(I32), x_words[0].rearrange("p c r -> p (c r)").bitcast(I32)
+        )
+        for tile, src in zip(places, (pos1, pos2, pos3)):
+            nc.sync.dma_start(tile[:], src)
+
+        x_scale = sbuf([P, S], U8, "x_scale")
+        nc.vector.tensor_copy(x_scale[:], table_scales[:].indirect(picked[:]))
+
+        w_round = [sbuf([P, PACK, HALF_P, PACK], BF16, "w_round%d" % h) for h in range(2)]
+        w_code = [sbuf([P, P], U32, "w_code%d" % t) for t in range(PACK)]
+        w_scale = [sbuf([P, P], U8, "w_scale%d" % t) for t in range(PACK)]
+
+        def round_views(h, lo, hi):
+            dst = w_round[h][:].rearrange("p t m j -> p m j t")[:, lo:hi]
+            src = w_raw[h][:].rearrange("p j (m t) -> p m j t", t=PACK)[:, lo:hi]
+            return dst, src
+
+        def quantise_w(h):
+            cols = slice(h * HALF_P, (h + 1) * HALF_P)
+            for t in range(PACK):
+                nc.vector.quantize_mx(
+                    out=w_code[t][:, cols].bitcast(FP8X4),
+                    scales=w_scale[t][:, cols],
+                    in_=w_round[h][:, t].rearrange("p m j -> p (m j)"),
+                )
+
+        dst, src = round_views(0, 0, HALF_P)
+        nc.scalar.activation(dst, src, COPY)
+        dst, src = round_views(1, 0, VECTOR_SHARE)
+        nc.vector.tensor_copy(dst, src)
+        dst, src = round_views(1, VECTOR_SHARE, HALF_P)
+        nc.scalar.activation(dst, src, COPY)
+        quantise_w(0)
+        quantise_w(1)
+
+        x_code = [sbuf([P, HALF_S], U32, "x_code%d" % h) for h in range(2)]
+        for h in range(2):
+            cols = HALF_S // LANES
+            nc.vector.tensor_copy(
+                x_code[h][:], table_words[:].indirect(picked[:, h * cols : (h + 1) * cols])
+            )
+
+        y = [sbuf([P, S], F32, "y%d" % t) for t in range(PACK)]
+        for t, h in ((0, 0), (1, 0), (0, 1), (1, 1), (2, 0), (2, 1), (3, 0), (3, 1)):
+            entries = slice(h * HALF_S, (h + 1) * HALF_S)
+            acc = psum.tile([P, HALF_S], F32, name="acc%d%d" % (t, h))
+            nc.tensor.matmul_mx(
+                out=acc[:],
+                lhsT=w_code[t][:].bitcast(FP8X4),
+                lhsT_scale=w_scale[t][:],
+                rhs=x_code[h][:].bitcast(FP8X4),
+                rhs_scale=x_scale[:, entries],
+                start=True,
+                stop=True,
+            )
+            if (t, h) == (0, 1):
+                nc.vector.tensor_copy(y[t][:, entries], acc[:])
+            else:
+                nc.scalar.copy(y[t][:, entries], acc[:])
+
+        def stage(name, dtype=F32):
+            return [sbuf([P, PACK, HALF_V], dtype, "%s%d" % (name, g)) for g in range(2)]
+
+        near = [stage("near%d_" % i) for i in range(3)]
+        low, high, capped, median = stage("low"), stage("high"), stage("capped"), stage("median")
+        rounded = [sbuf([P, HALF_V, PACK], BF16, "rounded%d" % g) for g in range(2)]
+        out_code = [sbuf([P, HALF_V], U32, "out_code%d" % g) for g in range(2)]
+        out_scale = sbuf([P, V], U8, "out_scale")
+        out_rows = out_0.rearrange("(p t) v -> p t v", t=PACK)
+        out_words = out_1[0].rearrange("p c r -> p (c r)").bitcast(I32)
+
+        def fetch(g, pair, on_vector):
+            cols = HALF_V // LANES
+            first, second = 2 * pair, 2 * pair + 1
+            for i, t in ((0, first), (1, first), (0, second), (1, second), (2, first), (2, second)):
+                window = y[t][:].indirect(places[i][:, g * cols : (g + 1) * cols])
+                if on_vector:
+                    nc.vector.tensor_copy(near[i][g][:, t, :], window)
+                else:
+                    nc.scalar.activation(near[i][g][:, t, :], window, COPY)
+
+        def op(out, a, b, alu, g, ts):
+            nc.vector.tensor_tensor(out[g][:, ts, :], a[g][:, ts, :], b[g][:, ts, :], alu)
+
+        def upper(g, ts):
+            op(high, near[0], near[1], MAX, g, ts)
+
+        def lower(g, ts):
+            op(low, near[0], near[1], MIN, g, ts)
+
+        def cap(g, ts):
+            op(capped, high, near[2], MIN, g, ts)
+
+        def finish(g, ts):
+            op(median, low, capped, MAX, g, ts)
+
+        def round_out(g, lo, hi, on_vector):
+            dst = rounded[g][:, lo:hi, :].rearrange("p (c i) t -> p c t i", i=PACK)
+            src = median[g][:, :, lo:hi].rearrange("p t (c i) -> p c t i", i=PACK)
+            if on_vector:
+                nc.vector.tensor_copy(dst, src)
+            else:
+                nc.scalar.copy(dst, src)
+
+        def quantise_out(g, lo, hi):
+            nc.vector.quantize_mx(
+                out=out_code[g][:, lo:hi].bitcast(FP8X4),
+                scales=out_scale[:, g * HALF_V + lo : g * HALF_V + hi],
+                in_=rounded[g][:, lo:hi, :].rearrange("p v t -> p (v t)"),
+            )
+
+        def store_values(g):
+            nc.sync.dma_start(out_rows[:, :, g * HALF_V : (g + 1) * HALF_V], median[g][:])
+
+        def store_words(g):
+            nc.sync.dma_start(
+                out_words[:, g * HALF_V : (g + 1) * HALF_V], out_code[g][:].bitcast(I32)
+            )
+
+        front, back = slice(0, 2), slice(2, 4)
+        fetch(0, 0, True)
+        fetch(0, 1, False)
+        fetch(1, 0, False)
+        fetch(1, 1, False)
+        upper(0, front)
+        lower(0, front)
+        cap(0, front)
+        upper(0, back)
+        finish(0, front)
+        lower(0, back)
+        cap(0, back)
+        upper(1, front)
+        finish(0, back)
+        store_values(0)
+        lower(1, front)
+        round_out(0, 0, HALF_V, True)
+        cap(1, front)
+        quantise_out(0, 0, HALF_V)
+        store_words(0)
+        finish(1, front)
+        upper(1, back)
+        lower(1, back)
+        for step in (cap, finish):
+            for t in (2, 3):
+                step(1, slice(t, t + 1))
+        store_values(1)
+        round_out(1, 0, HALF_V // 2, True)
+        round_out(1, HALF_V // 2, HALF_V, False)
+        quantise_out(1, 0, HALF_V // 2)
+        quantise_out(1, HALF_V // 2, HALF_V)
+        store_words(1)
+        for q in range(4):
+            queue = nc.scalar if q % 2 else nc.sync
+            queue.dma_start(
+                out_2[0, 4 * q : 4 * q + 4, :].bitcast(I32),
+                out_scale[32 * q : 32 * q + 4, :].bitcast(I32),
+            )

@@ -34,8 +34,8 @@ def tile_picked_median_none_po_kernel(
         keep = ctx.enter_context(tc.tile_pool(name="keep", bufs=1))
         psum = ctx.enter_context(tc.psum_pool(name="psum", bufs=1))
 
-        def sbuf(shape, dtype, name):
-            return keep.tile(shape, dtype, name=name, align_bytes=64)
+        def sbuf(shape, dtype, name, tag=None):
+            return keep.tile(shape, dtype, name=name, tag=tag or name, align_bytes=64)
 
         picked = keep.tile([P, S // LANES], U16, name="picked")
         places = [keep.tile([P, V // LANES], U16, name="places%d" % i) for i in range(3)]
@@ -63,7 +63,6 @@ def tile_picked_median_none_po_kernel(
         nc.vector.tensor_copy(x_scale[:], table_scales[:].indirect(picked[:]))
 
         w_round = [sbuf([P, PACK, HALF_P, PACK], BF16, "w_round%d" % h) for h in range(2)]
-        w_code = [sbuf([P, P], U32, "w_code%d" % t) for t in range(PACK)]
         w_scale = [sbuf([P, P], U8, "w_scale%d" % t) for t in range(PACK)]
 
         def round_views(h, lo, hi):
@@ -71,14 +70,16 @@ def tile_picked_median_none_po_kernel(
             src = w_raw[h][:].rearrange("p j (m t) -> p m j t", t=PACK)[:, lo:hi]
             return dst, src
 
-        def quantise_w(h):
-            cols = slice(h * HALF_P, (h + 1) * HALF_P)
-            for t in range(PACK):
-                nc.vector.quantize_mx(
-                    out=w_code[t][:, cols].bitcast(FP8X4),
-                    scales=w_scale[t][:, cols],
-                    in_=w_round[h][:, t].rearrange("p m j -> p (m j)"),
-                )
+        def quantise_w(codes, pair):
+            for u in range(2):
+                t = 2 * pair + u
+                for h in range(2):
+                    cols = slice(h * HALF_P, (h + 1) * HALF_P)
+                    nc.vector.quantize_mx(
+                        out=codes[:, u, cols].bitcast(FP8X4),
+                        scales=w_scale[t][:, cols],
+                        in_=w_round[h][:, t].rearrange("p m j -> p (m j)"),
+                    )
 
         dst, src = round_views(0, 0, HALF_P)
         nc.scalar.activation(dst, src, COPY)
@@ -86,125 +87,135 @@ def tile_picked_median_none_po_kernel(
         nc.vector.tensor_copy(dst, src)
         dst, src = round_views(1, VECTOR_SHARE, HALF_P)
         nc.scalar.activation(dst, src, COPY)
-        quantise_w(0)
-        quantise_w(1)
+        front_code = sbuf([P, 2, P], U32, "front_code")
+        quantise_w(front_code, 0)
 
-        x_code = [sbuf([P, HALF_S], U32, "x_code%d" % h) for h in range(2)]
+        x_code = sbuf([P, S], U32, "x_code")
         for h in range(2):
             cols = HALF_S // LANES
             nc.vector.tensor_copy(
-                x_code[h][:], table_words[:].indirect(picked[:, h * cols : (h + 1) * cols])
+                x_code[:, h * HALF_S : (h + 1) * HALF_S],
+                table_words[:].indirect(picked[:, h * cols : (h + 1) * cols]),
             )
 
+        back_code = sbuf([P, 2, P], U32, "back_code", tag="table_words")
+        quantise_w(back_code, 1)
+        w_code = (front_code, back_code)
+
         y = [sbuf([P, S], F32, "y%d" % t) for t in range(PACK)]
-        for t, h in ((0, 0), (1, 0), (0, 1), (1, 1), (2, 0), (2, 1), (3, 0), (3, 1)):
-            entries = slice(h * HALF_S, (h + 1) * HALF_S)
-            acc = psum.tile([P, HALF_S], F32, name="acc%d%d" % (t, h))
+
+        def product(t, lo, hi, on_vector):
+            acc = psum.tile([P, hi - lo], F32, name="acc%d_%d" % (t, lo))
             nc.tensor.matmul_mx(
                 out=acc[:],
-                lhsT=w_code[t][:].bitcast(FP8X4),
+                lhsT=w_code[t // 2][:, t % 2, :].bitcast(FP8X4),
                 lhsT_scale=w_scale[t][:],
-                rhs=x_code[h][:].bitcast(FP8X4),
-                rhs_scale=x_scale[:, entries],
+                rhs=x_code[:, lo:hi].bitcast(FP8X4),
+                rhs_scale=x_scale[:, lo:hi],
                 start=True,
                 stop=True,
             )
-            if (t, h) == (0, 1):
-                nc.vector.tensor_copy(y[t][:, entries], acc[:])
-            else:
-                nc.scalar.copy(y[t][:, entries], acc[:])
+            return lambda: (nc.vector.tensor_copy if on_vector else nc.scalar.copy)(
+                y[t][:, lo:hi], acc[:]
+            )
 
-        def stage(name, dtype=F32):
-            return [sbuf([P, PACK, HALF_V], dtype, "%s%d" % (name, g)) for g in range(2)]
+        def stage(name):
+            return sbuf([P, PACK, V], F32, name)
 
-        near = [stage("near%d_" % i) for i in range(3)]
+        near = [stage("near%d" % i) for i in range(3)]
         low, high, capped, median = stage("low"), stage("high"), stage("capped"), stage("median")
-        rounded = [sbuf([P, HALF_V, PACK], BF16, "rounded%d" % g) for g in range(2)]
-        out_code = [sbuf([P, HALF_V], U32, "out_code%d" % g) for g in range(2)]
+        rounded = sbuf([P, V, PACK], BF16, "rounded")
+        out_code = sbuf([P, V], U32, "out_code")
         out_scale = sbuf([P, V], U8, "out_scale")
         out_rows = out_0.rearrange("(p t) v -> p t v", t=PACK)
         out_words = out_1[0].rearrange("p c r -> p (c r)").bitcast(I32)
 
-        def fetch(g, pair, on_vector):
-            cols = HALF_V // LANES
-            first, second = 2 * pair, 2 * pair + 1
-            for i, t in ((0, first), (1, first), (0, second), (1, second), (2, first), (2, second)):
-                window = y[t][:].indirect(places[i][:, g * cols : (g + 1) * cols])
-                if on_vector:
-                    nc.vector.tensor_copy(near[i][g][:, t, :], window)
-                else:
-                    nc.scalar.activation(near[i][g][:, t, :], window, COPY)
+        def fetch(i, t, vs, on_vector):
+            window = y[t][:].indirect(places[i][:, vs.start // LANES : vs.stop // LANES])
+            if on_vector:
+                nc.vector.tensor_copy(near[i][:, t, vs], window)
+            else:
+                nc.scalar.activation(near[i][:, t, vs], window, COPY)
 
-        def op(out, a, b, alu, g, ts):
-            nc.vector.tensor_tensor(out[g][:, ts, :], a[g][:, ts, :], b[g][:, ts, :], alu)
+        def op(out, a, b, alu, ts, vs):
+            nc.vector.tensor_tensor(out[:, ts, vs], a[:, ts, vs], b[:, ts, vs], alu)
 
-        def upper(g, ts):
-            op(high, near[0], near[1], MAX, g, ts)
+        def upper(ts, vs):
+            op(high, near[0], near[1], MAX, ts, vs)
 
-        def lower(g, ts):
-            op(low, near[0], near[1], MIN, g, ts)
+        def lower(ts, vs):
+            op(low, near[0], near[1], MIN, ts, vs)
 
-        def cap(g, ts):
-            op(capped, high, near[2], MIN, g, ts)
+        def cap(ts, vs):
+            op(capped, high, near[2], MIN, ts, vs)
 
-        def finish(g, ts):
-            op(median, low, capped, MAX, g, ts)
+        def finish(ts, vs):
+            op(median, low, capped, MAX, ts, vs)
 
-        def round_out(g, lo, hi, on_vector):
-            dst = rounded[g][:, lo:hi, :].rearrange("p (c i) t -> p c t i", i=PACK)
-            src = median[g][:, :, lo:hi].rearrange("p t (c i) -> p c t i", i=PACK)
+        def round_out(vs, on_vector):
+            dst = rounded[:, vs, :].rearrange("p (c i) t -> p c t i", i=PACK)
+            src = median[:, :, vs].rearrange("p t (c i) -> p c t i", i=PACK)
             if on_vector:
                 nc.vector.tensor_copy(dst, src)
             else:
                 nc.scalar.copy(dst, src)
 
-        def quantise_out(g, lo, hi):
+        def quantise_out(vs):
             nc.vector.quantize_mx(
-                out=out_code[g][:, lo:hi].bitcast(FP8X4),
-                scales=out_scale[:, g * HALF_V + lo : g * HALF_V + hi],
-                in_=rounded[g][:, lo:hi, :].rearrange("p v t -> p (v t)"),
+                out=out_code[:, vs].bitcast(FP8X4),
+                scales=out_scale[:, vs],
+                in_=rounded[:, vs, :].rearrange("p v t -> p (v t)"),
             )
 
-        def store_values(g):
-            nc.sync.dma_start(out_rows[:, :, g * HALF_V : (g + 1) * HALF_V], median[g][:])
+        def store_values(ts, vs):
+            nc.sync.dma_start(out_rows[:, ts, vs], median[:, ts, vs])
 
-        def store_words(g):
-            nc.sync.dma_start(
-                out_words[:, g * HALF_V : (g + 1) * HALF_V], out_code[g][:].bitcast(I32)
-            )
+        def store_words(vs):
+            nc.sync.dma_start(out_words[:, vs], out_code[:, vs].bitcast(I32))
 
         front, back = slice(0, 2), slice(2, 4)
-        fetch(0, 0, True)
-        fetch(0, 1, False)
-        fetch(1, 0, False)
-        fetch(1, 1, False)
-        upper(0, front)
-        lower(0, front)
-        cap(0, front)
-        upper(0, back)
-        finish(0, front)
-        lower(0, back)
-        cap(0, back)
-        upper(1, front)
-        finish(0, back)
-        store_values(0)
-        lower(1, front)
-        round_out(0, 0, HALF_V, True)
-        cap(1, front)
-        quantise_out(0, 0, HALF_V)
-        store_words(0)
-        finish(1, front)
-        upper(1, back)
-        lower(1, back)
+        whole, early, late = slice(0, V), slice(0, HALF_V), slice(HALF_V, V)
+        third, fourth = slice(HALF_V, HALF_V + V // 4), slice(HALF_V + V // 4, V)
+
+        product(0, 0, HALF_S, False)()
+        product(1, 0, HALF_S, False)()
+        product(0, HALF_S, S, True)()
+        product(1, HALF_S, S, False)()
+        copy_back = [product(t, 0, S, False) for t in (2, 3)]
+        for i in range(3):
+            fetch(i, 0, whole, True)
+        fetch(0, 1, whole, True)
+        fetch(1, 1, whole, False)
+        fetch(2, 1, whole, False)
+        for copy_out in copy_back:
+            copy_out()
+        for vs in (early, late):
+            for i, t in ((0, 2), (1, 2), (0, 3), (1, 3), (2, 2), (2, 3)):
+                fetch(i, t, vs, False)
+        upper(front, whole)
+        lower(front, whole)
+        cap(front, whole)
+        upper(back, early)
+        finish(front, whole)
+        store_values(front, whole)
+        lower(back, early)
+        cap(back, early)
+        upper(back, late)
+        finish(back, early)
+        store_values(back, early)
+        round_out(early, False)
+        lower(back, late)
         for step in (cap, finish):
             for t in (2, 3):
-                step(1, slice(t, t + 1))
-        store_values(1)
-        round_out(1, 0, HALF_V // 2, True)
-        round_out(1, HALF_V // 2, HALF_V, False)
-        quantise_out(1, 0, HALF_V // 2)
-        quantise_out(1, HALF_V // 2, HALF_V)
-        store_words(1)
+                step(slice(t, t + 1), late)
+        store_values(back, late)
+        quantise_out(early)
+        store_words(early)
+        round_out(third, True)
+        round_out(fourth, False)
+        quantise_out(third)
+        quantise_out(fourth)
+        store_words(late)
         for q in range(4):
             queue = nc.scalar if q % 2 else nc.sync
             queue.dma_start(

from contextlib import ExitStack

import concourse.mybir as mybir

K, T, S, V, N = 512, 1024, 512, 256, 512
FLOPS = 2 * K * N * S

F32 = mybir.dt.float32
BF16 = mybir.dt.bfloat16
I32 = mybir.dt.int32
U32 = mybir.dt.uint32
U16 = mybir.dt.uint16
U8 = mybir.dt.uint8
FP8X4 = mybir.dt.float8_e4m3fn_x4
COPY = mybir.ActivationFunctionType.Copy
MAX = mybir.AluOpType.max
MIN = mybir.AluOpType.min

P = 128
PACK = 4
LANES = 16
HALF_S = S // 2
HALF_N = N // 2
HALF_P = P // 2
HALF_V = V // 2
VECTOR_SHARE = 40


def tile_picked_median_none_po_kernel(
    tc, x_words, x_scales, w1, offs, pos1, pos2, pos3, out_0, out_1, out_2
):
    nc = tc.nc
    with ExitStack() as ctx:
        keep = ctx.enter_context(tc.tile_pool(name="keep", bufs=1))
        psum = ctx.enter_context(tc.psum_pool(name="psum", bufs=1))

        def sbuf(shape, dtype, name, tag=None):
            return keep.tile(shape, dtype, name=name, tag=tag or name, align_bytes=64)

        picked = keep.tile([P, S // LANES], U16, name="picked")
        places = [keep.tile([P, V // LANES], U16, name="places%d" % i) for i in range(3)]
        table_words = sbuf([P, T], U32, "table_words")
        table_scales = sbuf([P, T], U8, "table_scales")
        w_raw = [sbuf([P, PACK, HALF_N], F32, "w_raw%d" % h) for h in range(2)]

        nc.vector.memset(table_scales[:].bitcast(I32), 0)
        nc.sync.dma_start(picked[:], offs)
        w_rows = w1.rearrange("(p j) c -> p j c", j=PACK)
        nc.sync.dma_start(w_raw[0][:], w_rows[:, :, :HALF_N])
        for q in range(4):
            nc.sync.dma_start(
                table_scales[32 * q : 32 * q + 4, :].bitcast(I32),
                x_scales[0, 4 * q : 4 * q + 4, :].bitcast(I32),
            )
        nc.sync.dma_start(w_raw[1][:], w_rows[:, :, HALF_N:])
        nc.sync.dma_start(
            table_words[:].bitcast(I32), x_words[0].rearrange("p c r -> p (c r)").bitcast(I32)
        )
        for tile, src in zip(places, (pos1, pos2, pos3)):
            nc.sync.dma_start(tile[:], src)

        x_scale = sbuf([P, S], U8, "x_scale")
        nc.vector.tensor_copy(x_scale[:], table_scales[:].indirect(picked[:]))

        w_round = [sbuf([P, PACK, HALF_P, PACK], BF16, "w_round%d" % h) for h in range(2)]
        w_scale = [sbuf([P, P], U8, "w_scale%d" % t) for t in range(PACK)]

        def round_views(h, lo, hi):
            dst = w_round[h][:].rearrange("p t m j -> p m j t")[:, lo:hi]
            src = w_raw[h][:].rearrange("p j (m t) -> p m j t", t=PACK)[:, lo:hi]
            return dst, src

        def quantise_w(codes, pair):
            for u in range(2):
                t = 2 * pair + u
                for h in range(2):
                    cols = slice(h * HALF_P, (h + 1) * HALF_P)
                    nc.vector.quantize_mx(
                        out=codes[:, u, cols].bitcast(FP8X4),
                        scales=w_scale[t][:, cols],
                        in_=w_round[h][:, t].rearrange("p m j -> p (m j)"),
                    )

        dst, src = round_views(0, 0, HALF_P)
        nc.scalar.activation(dst, src, COPY)
        dst, src = round_views(1, 0, VECTOR_SHARE)
        nc.vector.tensor_copy(dst, src)
        dst, src = round_views(1, VECTOR_SHARE, HALF_P)
        nc.scalar.activation(dst, src, COPY)
        front_code = sbuf([P, 2, P], U32, "front_code")
        quantise_w(front_code, 0)

        x_code = sbuf([P, S], U32, "x_code")
        for h in range(2):
            cols = HALF_S // LANES
            nc.vector.tensor_copy(
                x_code[:, h * HALF_S : (h + 1) * HALF_S],
                table_words[:].indirect(picked[:, h * cols : (h + 1) * cols]),
            )

        back_code = sbuf([P, 2, P], U32, "back_code", tag="table_words")
        quantise_w(back_code, 1)
        w_code = (front_code, back_code)

        y = [sbuf([P, S], F32, "y%d" % t) for t in range(PACK)]

        def product(t, lo, hi, on_vector):
            acc = psum.tile([P, hi - lo], F32, name="acc%d_%d" % (t, lo))
            nc.tensor.matmul_mx(
                out=acc[:],
                lhsT=w_code[t // 2][:, t % 2, :].bitcast(FP8X4),
                lhsT_scale=w_scale[t][:],
                rhs=x_code[:, lo:hi].bitcast(FP8X4),
                rhs_scale=x_scale[:, lo:hi],
                start=True,
                stop=True,
            )
            return lambda: (nc.vector.tensor_copy if on_vector else nc.scalar.copy)(
                y[t][:, lo:hi], acc[:]
            )

        def stage(name):
            return sbuf([P, PACK, V], F32, name)

        near = [stage("near%d" % i) for i in range(3)]
        low, high, capped, median = stage("low"), stage("high"), stage("capped"), stage("median")
        rounded = sbuf([P, V, PACK], BF16, "rounded")
        out_code = sbuf([P, V], U32, "out_code")
        out_scale = sbuf([P, V], U8, "out_scale")
        out_rows = out_0.rearrange("(p t) v -> p t v", t=PACK)
        out_words = out_1[0].rearrange("p c r -> p (c r)").bitcast(I32)

        def fetch(i, t, vs, on_vector):
            window = y[t][:].indirect(places[i][:, vs.start // LANES : vs.stop // LANES])
            if on_vector:
                nc.vector.tensor_copy(near[i][:, t, vs], window)
            else:
                nc.scalar.activation(near[i][:, t, vs], window, COPY)

        def op(out, a, b, alu, ts, vs):
            nc.vector.tensor_tensor(out[:, ts, vs], a[:, ts, vs], b[:, ts, vs], alu)

        def upper(ts, vs):
            op(high, near[0], near[1], MAX, ts, vs)

        def lower(ts, vs):
            op(low, near[0], near[1], MIN, ts, vs)

        def cap(ts, vs):
            op(capped, high, near[2], MIN, ts, vs)

        def finish(ts, vs):
            op(median, low, capped, MAX, ts, vs)

        def round_out(vs, on_vector):
            dst = rounded[:, vs, :].rearrange("p (c i) t -> p c t i", i=PACK)
            src = median[:, :, vs].rearrange("p t (c i) -> p c t i", i=PACK)
            if on_vector:
                nc.vector.tensor_copy(dst, src)
            else:
                nc.scalar.copy(dst, src)

        def quantise_out(vs):
            nc.vector.quantize_mx(
                out=out_code[:, vs].bitcast(FP8X4),
                scales=out_scale[:, vs],
                in_=rounded[:, vs, :].rearrange("p v t -> p (v t)"),
            )

        def store_values(ts, vs):
            nc.sync.dma_start(out_rows[:, ts, vs], median[:, ts, vs])

        def store_words(vs):
            nc.sync.dma_start(out_words[:, vs], out_code[:, vs].bitcast(I32))

        front, back = slice(0, 2), slice(2, 4)
        whole, early, late = slice(0, V), slice(0, HALF_V), slice(HALF_V, V)
        third, fourth = slice(HALF_V, HALF_V + V // 4), slice(HALF_V + V // 4, V)

        product(0, 0, HALF_S, False)()
        product(1, 0, HALF_S, False)()
        product(0, HALF_S, S, True)()
        product(1, HALF_S, S, False)()
        copy_back = [product(t, 0, S, False) for t in (2, 3)]
        for i in range(3):
            fetch(i, 0, whole, True)
        fetch(0, 1, whole, True)
        fetch(1, 1, whole, False)
        fetch(2, 1, whole, False)
        for copy_out in copy_back:
            copy_out()
        for vs in (early, late):
            for i, t in ((0, 2), (1, 2), (0, 3), (1, 3), (2, 2), (2, 3)):
                fetch(i, t, vs, False)
        upper(front, whole)
        lower(front, whole)
        cap(front, whole)
        upper(back, early)
        finish(front, whole)
        store_values(front, whole)
        lower(back, early)
        cap(back, early)
        upper(back, late)
        finish(back, early)
        store_values(back, early)
        round_out(early, False)
        lower(back, late)
        for step in (cap, finish):
            for t in (2, 3):
                step(slice(t, t + 1), late)
        store_values(back, late)
        quantise_out(early)
        store_words(early)
        round_out(third, True)
        round_out(fourth, False)
        quantise_out(third)
        quantise_out(fourth)
        store_words(late)
        for q in range(4):
            queue = nc.scalar if q % 2 else nc.sync
            queue.dma_start(
                out_2[0, 4 * q : 4 * q + 4, :].bitcast(I32),
                out_scale[32 * q : 32 * q + 4, :].bitcast(I32),
            )
